import numpy as np
import ml_dtypes


def mxq(x, axis, fmt="e4m3"):
    dtype, down = {"e4m3": (ml_dtypes.float8_e4m3fn, 7), "e5m2": (ml_dtypes.float8_e5m2, 14)}[fmt]
    v = np.moveaxis(np.asarray(x, np.float32).astype(ml_dtypes.bfloat16).astype(np.float64), axis, -1)
    blocks = v.reshape(v.shape[:-1] + (-1, 32))
    amax = np.abs(blocks).max(-1, keepdims=True)
    byte = np.maximum(np.where(amax > 0, np.frexp(amax)[1] - 1 + 127, 0) - down, 1)
    scale = np.exp2(byte - 127.0)
    codes = (blocks / scale).astype(np.float32).astype(dtype).astype(np.float64)
    return np.moveaxis((codes * scale).reshape(v.shape), -1, axis)


WIDE = False


def mx_kscale(k):
    if not WIDE:
        return np.ones(k)
    levels = np.array([10, -10, 5, -5, 0])
    if k % 512:
        return np.exp2(np.random.permutation(np.resize(levels, k // 32))).repeat(32)
    a = np.empty((k // 512, 16))
    for p in range(k // 512):
        a[p, :8] = np.random.permutation(np.resize(levels, 8))
        for g in range(8):
            far = levels[np.abs(levels - a[p, g]) >= 10]
            a[p, g + 8] = far[np.random.randint(len(far))]
    return np.exp2(a.ravel()).repeat(32)


BF16 = ml_dtypes.bfloat16


def bf(x):
    return np.asarray(x, np.float32).astype(BF16)


def f64(x):
    return np.asarray(x).astype(np.float64)


B, D, K, M, T = 1024, 1024, 2, 512, 2
H = K * M


def sigmoid(v):
    return 1.0 / (1.0 + np.exp(-v))


def draw0():
    c = mx_kscale(D)
    t = mx_kscale(H)
    return {
        "x": bf(np.random.standard_normal((B, D)) * c),
        "s": bf(np.random.standard_normal((T, D))),
        "w1": bf(np.random.standard_normal((D, H)) / np.sqrt(D) / c[:, None]),
        "w2": bf(np.random.standard_normal((D, H)) / np.sqrt(D) / c[:, None]),
        "r": bf(np.random.standard_normal(H) * t),
        "wf": bf(1.5 * np.random.standard_normal((K, M, M)) / np.sqrt(M) / t.reshape(K, M)[:, :, None]),
        "a": bf(np.random.standard_normal((T, H)) * 0.7),
    }


def gated_stream(x, logits, w):
    gated = x * (2.0 * sigmoid(logits))
    return np.maximum(mxq(gated, 1, "e4m3") @ mxq(w, 0, "e4m3"), 0.0)


def headwise_product(u, wf):
    heads, width, _ = wf.shape
    u_heads = u.reshape(u.shape[0], heads, width).transpose(1, 0, 2)
    f_heads = mxq(u_heads, 2, "e4m3") @ mxq(wf, 1, "e4m3")
    return f_heads.transpose(1, 0, 2).reshape(u.shape)


def core(x, s, w1, w2, r, wf, a):
    x, s, w1, w2, r, wf, a = f64(x), f64(s), f64(w1), f64(w2), f64(r), f64(wf), f64(a)
    o1 = gated_stream(x, s[0], w1)
    o2 = gated_stream(x, s[1], w2)
    u = o1 * r
    f = headwise_product(u, wf)
    return (f + a[1]) * o2 + a[0] * o1


def e4m3fn_bytes(y):
    return np.clip(np.asarray(y, np.float64), -448.0, 448.0).astype(np.float32).astype(ml_dtypes.float8_e4m3fn).view(np.uint8)


def e4m3fn_values(b):
    return np.asarray(b, np.uint8).view(ml_dtypes.float8_e4m3fn).astype(np.float64)


def setup_inputs():
    d = draw0()
    x0 = np.asarray(d['w2']).astype(np.float64)
    s = (np.max(np.abs(x0), axis=(1,), keepdims=True) / 448.0).astype(np.float32)
    out = {}
    for k, v in d.items():
        if k == 'w2':
            out['w2_bytes'] = e4m3fn_bytes(x0 / s.astype(np.float64))
            out['w2_scale'] = s
        else:
            out[k] = v
    return out


def reference(x, s, w1, w2_bytes, w2_scale, r, wf, a):
    return core(x, s, w1, e4m3fn_values(w2_bytes) * w2_scale.astype(np.float64), r, wf, a)

@@ -1,0 +1,458 @@
+from contextlib import ExitStack
+
+import concourse.mybir as mybir
+from concourse.masks import make_identity
+
+F32 = mybir.dt.float32
+BF16 = mybir.dt.bfloat16
+U32 = mybir.dt.uint32
+U8 = mybir.dt.uint8
+FP8 = mybir.dt.float8_e4m3fn
+X4 = mybir.dt.float8_e4m3fn_x4
+ALU = mybir.AluOpType
+ACT = mybir.ActivationFunctionType
+
+B, D, HEADS, W = 1024, 1024, 2, 512
+H = HEADS * W
+FLOPS = 2 * (2 * B * D * H + HEADS * B * W * W)
+
+P = 128
+PASSES = D // 512
+TB = 256
+NB = B // TB
+TT = TB // P
+ON_GPSIMD = (("wf", 0, 0), ("wf", 1, 0), ("w2", 0, 0), ("w2", 1, 0), ("w2", 0, 1), ("w2", 1, 1))
+SPLIT = ((0, 0), (0, 1), (1, 0), (1, 1), (2, 0), (2, 1), (3, 0), (3, 1))
+
+
+def tile_finalmlptwostreamfusion_kernel(tc, x, s, w1, w2_bytes, w2_scale, r, wf, a, out):
+    nc = tc.nc
+    with ExitStack() as ctx:
+        keep = ctx.enter_context(tc.tile_pool(name="keep", bufs=1))
+        work = ctx.enter_context(tc.tile_pool(name="work", bufs=1))
+        psum = ctx.enter_context(tc.psum_pool(name="psum", bufs=1))
+
+        ident = keep.tile([P, P], F32, name="ident")
+        make_identity(nc, ident[:])
+
+        ctx.enter_context(tc.manual_schedule())
+
+        s_bf = keep.tile([P, 2 * PASSES, 4], BF16, name="s_bf")
+        nc.scalar.dma_start(out=s_bf[:], in_=s.rearrange("k (g p t) -> p (k g) t", p=P, t=4))
+        ws = keep.tile([P, PASSES, 4], F32, name="ws")
+        nc.scalar.dma_start(out=ws[:], in_=w2_scale.rearrange("(g p t) o -> p g (t o)", p=P, t=4))
+        r_bf = keep.tile([P, HEADS, 4], BF16, name="r_bf")
+        nc.scalar.dma_start(out=r_bf[:], in_=r.rearrange("(h p t) -> p h t", p=P, t=4))
+        a_bf = keep.tile([P, 2 * HEADS, 4], BF16, name="a_bf")
+        nc.scalar.dma_start(out=a_bf[:], in_=a.rearrange("k (h p t) -> p (k h) t", p=P, t=4))
+
+        x_raw = [keep.tile([P, TT, D], BF16, name="x_raw%d" % b) for b in range(NB)]
+        w1_raw = [keep.tile([P, 4, H], BF16, name="w1_raw%d" % g) for g in range(PASSES)]
+        w2_raw = [keep.tile([P, 4, H], U8, name="w2_raw%d" % g) for g in range(PASSES)]
+        wf_raw = [keep.tile([P, 4, W], BF16, name="wf_raw%d" % h) for h in range(HEADS)]
+
+        def load_x(b):
+            nc.sync.dma_start(out=x_raw[b][:], in_=x[b * TB : (b + 1) * TB, :].rearrange("(i p) k -> p i k", p=P))
+
+        def load_w(dst, src):
+            nc.sync.dma_start(out=dst[:], in_=src.rearrange("(p j) n -> p j n", j=4))
+
+        load_x(0)
+        load_w(w1_raw[0], w1[0:512, :])
+        load_x(1)
+        load_w(w1_raw[1], w1[512:1024, :])
+        load_x(2)
+        load_w(w2_raw[0], w2_bytes[0:512, :])
+        load_x(3)
+        load_w(w2_raw[1], w2_bytes[512:1024, :])
+        load_w(wf_raw[0], wf[0])
+        load_w(wf_raw[1], wf[1])
+
+        sig = keep.tile([P, 2 * PASSES, 4], F32, name="sig")
+        nc.scalar.activation(out=sig[:], in_=s_bf[:], func=ACT.Sigmoid)
+        gate = keep.tile([P, 2 * PASSES, 4], F32, name="gate")
+        nc.vector.tensor_scalar(out=gate[:], in0=sig[:], scalar1=2.0, scalar2=None, op0=ALU.mult)
+        r_f = keep.tile([P, HEADS, 4], F32, name="r_f")
+        a_f = keep.tile([P, 2 * HEADS, 4], F32, name="a_f")
+
+        def widen_vectors():
+            nc.gpsimd.tensor_copy(out=r_f[:], in_=r_bf[:])
+            nc.gpsimd.tensor_copy(out=a_f[:], in_=a_bf[:])
+
+        def planes(n, name):
+            codes = keep.tile([P, 2, n], U32, name=name + "_c", align_bytes=64)
+            scales = keep.tile([P, 2, n], U8, name=name + "_s", align_bytes=64)
+            return codes, scales
+
+        w1_q = planes(H, "w1q")
+        w2_q = planes(H, "w2q")
+        wf_q = planes(W, "wfq")
+        g_q = []
+        for k in range(2):
+            codes = keep.tile([P, NB, PASSES, TB], U32, name="g%dq_c" % k, align_bytes=64)
+            scales = keep.tile([P, NB, PASSES, TB], U8, name="g%dq_s" % k, align_bytes=64)
+            g_q.append((codes, scales))
+        u_q = planes(B, "uq")
+
+        def quantize(q, index, lo, hi, grouped):
+            codes, scales = q
+            nc.vector.quantize_mx(out=codes[:, index, lo:hi].bitcast(X4), scales=scales[:, index, lo:hi], in_=grouped)
+
+        def mx(dst, lq, li, l0, rq, ri, r0, n, start, stop):
+            nc.tensor.matmul_mx(
+                out=dst,
+                lhsT=lq[0][:, li, l0 : l0 + P].bitcast(X4),
+                lhsT_scale=lq[1][:, li, l0 : l0 + P],
+                rhs=rq[0][:, ri, r0 : r0 + n].bitcast(X4),
+                rhs_scale=rq[1][:, ri, r0 : r0 + n],
+                start=start,
+                stop=stop,
+            )
+
+        xt = {}
+
+        def turn_x(b, g):
+            if True:
+                bank = psum.tile([P, 2, TB], F32, name="t_bank", bufs=3)
+                for u in range(2):
+                    for i in range(TT):
+                        words = x_raw[b][:, i, :].bitcast(F32)
+                        nc.tensor.transpose(
+                            bank[:, u, i * P : (i + 1) * P], words[:, 256 * g + u : 256 * (g + 1) : 2], ident[:]
+                        )
+                xt[b, g] = bank
+
+        xg = {}
+
+        def gate_x(b, g):
+            if (b, 0) not in xg:
+                for k in range(2):
+                    xg[b, k] = work.tile([P, PASSES, TB, 4], BF16, name="xg", bufs=4, align_bytes=64)
+            src = xt[b, g][:].bitcast(BF16).rearrange("p u (r e) -> p r u e", e=2)
+            if True:
+                for k in range(2):
+                    factor = gate[:, 2 * k + g, :].rearrange("p (u e) -> p u e", e=2).unsqueeze(1)
+                    nc.vector.tensor_tensor(
+                        out=xg[b, k][:, g, :, :].rearrange("p r (u e) -> p r u e", e=2),
+                        in0=src,
+                        in1=factor.to_broadcast([P, TB, 2, 2]),
+                        op=ALU.mult,
+                    )
+
+        def quant_x(b, k):
+            if True:
+                codes, scales = g_q[k]
+                nc.vector.quantize_mx(
+                    out=codes[:, b, :, :].rearrange("p g n -> p (g n)").bitcast(X4),
+                    scales=scales[:, b, :, :].rearrange("p g n -> p (g n)"),
+                    in_=xg[b, k][:].rearrange("p g r t -> p (g r t)"),
+                )
+
+        wg = {}
+
+        def group_w(tag, index, h, src):
+            tile = work.tile([P, 4 * W], BF16, name="wg", bufs=4, align_bytes=64)
+            dst = tile[:].rearrange("p (t m j) -> p t m j", t=4, j=4)
+            src = src.rearrange("p j (m t) -> p t m j", t=4)
+            if (tag, index, h) in ON_GPSIMD:
+                nc.gpsimd.tensor_scalar(out=dst, in0=src, scalar1=1.0, scalar2=0.0, op0=ALU.mult, op1=ALU.add)
+            else:
+                nc.scalar.copy(out=dst, in_=src)
+            wg[tag, index, h] = tile
+
+        def group_w1(h, g):
+            group_w("w1", g, h, w1_raw[g][:, :, h * W : (h + 1) * W])
+
+        def quant_w1(h, g):
+            quantize(w1_q, g, h * W, (h + 1) * W, wg["w1", g, h][:])
+
+        w2_wide = {}
+
+        def widen_w2(g, half):
+            if g not in w2_wide:
+                w2_wide[g] = work.tile([P, 4, H], BF16, name="big", bufs=3)
+            for j in (2 * half, 2 * half + 1):
+                nc.scalar.activation(
+                    out=w2_wide[g][:, j, :],
+                    in_=w2_raw[g][:, j, :].bitcast(FP8),
+                    func=ACT.Copy,
+                    scale=ws[:, g, j : j + 1],
+                )
+
+        def group_w2(h, g):
+            group_w("w2", g, h, w2_wide[g][:, :, h * W : (h + 1) * W])
+
+        def quant_w2(h, g):
+            quantize(w2_q, g, h * W, (h + 1) * W, wg["w2", g, h][:])
+
+        def group_wf(h):
+            group_w("wf", h, 0, wf_raw[h][:])
+
+        def quant_wf(h):
+            quantize(wf_q, h, 0, W, wg["wf", h, 0][:])
+
+        z1 = {}
+
+        def mul_z1(b, h):
+            for i in range(TT):
+                bank = psum.tile([P, 4, P], F32, name="z_bank", bufs=5)
+                for t in range(4):
+                    for g in range(PASSES):
+                        nc.tensor.matmul_mx(
+                            out=bank[:, t, :],
+                            lhsT=w1_q[0][:, g, h * W + t * P : h * W + (t + 1) * P].bitcast(X4),
+                            lhsT_scale=w1_q[1][:, g, h * W + t * P : h * W + (t + 1) * P],
+                            rhs=g_q[0][0][:, b, g, i * P : (i + 1) * P].bitcast(X4),
+                            rhs_scale=g_q[0][1][:, b, g, i * P : (i + 1) * P],
+                            start=(g == 0),
+                            stop=(g == PASSES - 1),
+                        )
+                z1[b, h, i] = bank
+
+        ug = {}
+        o1a = {}
+
+        def gain_z1(b, h):
+            ug[b, h] = work.tile([P, TT, P, 4], BF16, name="ug", bufs=3, align_bytes=64)
+            for i in range(TT):
+                nc.vector.scalar_tensor_tensor(
+                    out=ug[b, h][:, i, :, :],
+                    in0=z1[b, h, i][:].rearrange("p t n -> p n t"),
+                    scalar=0.0,
+                    in1=r_f[:, h, :].unsqueeze(1).to_broadcast([P, P, 4]),
+                    op0=ALU.max,
+                    op1=ALU.mult,
+                )
+
+        def linear_z1(b, h):
+            if b not in o1a:
+                o1a[b] = work.tile([P, HEADS, TT, 4, P], F32, name="o1a", bufs=3)
+            for i in range(TT):
+                if (b, h) in SPLIT:
+                    nc.scalar.activation(out=o1a[b][:, h, i, :, :], in_=z1[b, h, i][:], func=ACT.Relu)
+                else:
+                    nc.vector.scalar_tensor_tensor(
+                        out=o1a[b][:, h, i, :, :],
+                        in0=z1[b, h, i][:],
+                        scalar=0.0,
+                        in1=a_f[:, h, :].unsqueeze(2).to_broadcast([P, 4, P]),
+                        op0=ALU.max,
+                        op1=ALU.mult,
+                    )
+
+        def weigh_z1(b, h):
+            if (b, h) in SPLIT:
+                for t in range(4):
+                    part = o1a[b][:, h, :, t, :]
+                    nc.gpsimd.tensor_scalar(
+                        out=part, in0=part, scalar1=a_f[:, h, t : t + 1], scalar2=0.0, op0=ALU.mult, op1=ALU.add
+                    )
+
+        def quant_u(b, h):
+            quantize(u_q, h, b * TB, (b + 1) * TB, ug[b, h][:].rearrange("p i n t -> p (i n t)"))
+
+        z2 = {}
+        o2 = {}
+
+        def mul_z2(c, h):
+            for t in range(4):
+                bank = psum.tile([P, 2, TB], F32, name="z_bank", bufs=5)
+                for half in range(2):
+                    for g in range(PASSES):
+                        nc.tensor.matmul_mx(
+                            out=bank[:, half, :],
+                            lhsT=w2_q[0][:, g, h * W + t * P : h * W + (t + 1) * P].bitcast(X4),
+                            lhsT_scale=w2_q[1][:, g, h * W + t * P : h * W + (t + 1) * P],
+                            rhs=g_q[1][0][:, 2 * c + half, g, :].bitcast(X4),
+                            rhs_scale=g_q[1][1][:, 2 * c + half, g, :],
+                            start=(g == 0),
+                            stop=(g == PASSES - 1),
+                        )
+                z2[c, h, t] = bank
+
+        def use_z2(c, h):
+            if c not in o2:
+                o2[c] = work.tile([P, HEADS, 4, 2, TB], F32, name="o2", bufs=2)
+            for t in range(4):
+                nc.scalar.activation(out=o2[c][:, h, t, :, :], in_=z2[c, h, t][:], func=ACT.Relu)
+
+        fb = {}
+
+        def mul_f(b, h):
+            for tt in range(2):
+                bank = psum.tile([P, 2, TB], F32, name="z_bank", bufs=5)
+                for v in range(2):
+                    t = 2 * tt + v
+                    mx(bank[:, v, :], wf_q, h, t * P, u_q, h, b * TB, TB, True, True)
+                fb[b, h, tt] = bank
+
+        fused = {}
+
+        def fuse(b, h):
+            if b not in fused:
+                fused[b] = work.tile([P, HEADS, 4, TB], F32, name="big", bufs=3)
+            for t in range(4):
+                nc.vector.scalar_tensor_tensor(
+                    out=fused[b][:, h, t, :],
+                    in0=fb[b, h, t // 2][:, t % 2, :],
+                    scalar=a_f[:, HEADS + h, t : t + 1],
+                    in1=o2[b // 2][:, h, t, b % 2, :],
+                    op0=ALU.add,
+                    op1=ALU.mult,
+                )
+
+        tr = {}
+
+        def turn_out(b, h):
+            for i in range(TT):
+                bank = psum.tile([P, 4, P], F32, name="t_bank", bufs=3)
+                for t in range(4):
+                    nc.tensor.matmul(
+                        bank[:, t, :], lhsT=o1a[b][:, h, i, t, :], rhs=ident[:], start=True, stop=False, is_transpose=True
+                    )
+                    nc.tensor.matmul(
+                        bank[:, t, :],
+                        lhsT=fused[b][:, h, t, i * P : (i + 1) * P],
+                        rhs=ident[:],
+                        start=False,
+                        stop=True,
+                        is_transpose=True,
+                    )
+                tr[b, h, i] = bank
+
+        def store(b, h):
+            for i in range(TT):
+                rows = work.tile([P, W], F32, name="rows", bufs=6)
+                nc.scalar.copy(out=rows[:].rearrange("n (m t) -> n m t", t=4), in_=tr[b, h, i][:].rearrange("n t m -> n m t"))
+                n0 = b * TB + i * P
+                nc.sync.dma_start(out=out[n0 : n0 + P, h * W : (h + 1) * W], in_=rows[:])
+
+        turn_x(0, 1)
+        gate_x(0, 1)
+        turn_x(0, 0)
+        group_w1(1, 0)
+        turn_x(1, 0)
+        gate_x(0, 0)
+        turn_x(1, 1)
+        quant_x(0, 0)
+        group_w1(0, 0)
+        gate_x(1, 1)
+        quant_w1(1, 0)
+        turn_x(2, 1)
+        widen_vectors()
+        group_w1(0, 1)
+        gate_x(1, 0)
+        quant_w1(0, 1)
+        turn_x(2, 0)
+        quant_x(1, 1)
+        quant_w1(0, 0)
+        turn_x(3, 1)
+        mul_z1(0, 0)
+        widen_w2(1, 0)
+        widen_w2(1, 1)
+        quant_x(1, 0)
+        quant_x(0, 1)
+        gate_x(2, 1)
+        group_w1(1, 1)
+        group_w2(0, 1)
+        gain_z1(0, 0)
+        mul_z1(1, 0)
+        quant_w1(1, 1)
+        mul_z1(0, 1)
+        group_w2(1, 1)
+        linear_z1(0, 0)
+        group_wf(0)
+        gate_x(3, 1)
+        widen_w2(0, 0)
+        turn_x(3, 0)
+        gain_z1(0, 1)
+        widen_w2(0, 1)
+        mul_z1(1, 1)
+        linear_z1(0, 1)
+        gain_z1(1, 0)
+        group_w2(0, 0)
+        gate_x(2, 0)
+        group_w2(1, 0)
+        quant_w2(1, 1)
+        quant_u(1, 0)
+        quant_x(2, 0)
+        mul_z1(2, 0)
+        linear_z1(1, 0)
+        quant_u(0, 0)
+        mul_z1(2, 1)
+        quant_wf(0)
+        quant_u(0, 1)
+        weigh_z1(0, 0)
+        quant_w2(0, 1)
+        quant_w2(0, 0)
+        mul_z2(0, 0)
+        mul_f(0, 0)
+        gain_z1(1, 1)
+        gain_z1(2, 0)
+        gain_z1(2, 1)
+        linear_z1(1, 1)
+        quant_w2(1, 0)
+        mul_z2(0, 1)
+        group_wf(1)
+        weigh_z1(0, 1)
+        gate_x(3, 0)
+        linear_z1(2, 0)
+        linear_z1(2, 1)
+        use_z2(0, 0)
+        use_z2(0, 1)
+        fuse(0, 0)
+        turn_out(0, 0)
+        weigh_z1(1, 0)
+        quant_u(1, 1)
+        store(0, 0)
+        quant_wf(1)
+        mul_f(0, 1)
+        mul_f(1, 0)
+        quant_x(3, 0)
+        fuse(0, 1)
+        mul_z1(3, 0)
+        fuse(1, 0)
+        turn_out(0, 1)
+        quant_u(2, 0)
+        turn_out(1, 0)
+        quant_x(2, 1)
+        gain_z1(3, 0)
+        quant_x(3, 1)
+        store(0, 1)
+        mul_z1(3, 1)
+        mul_f(1, 1)
+        linear_z1(3, 0)
+        weigh_z1(3, 0)
+        weigh_z1(1, 1)
+        gain_z1(3, 1)
+        weigh_z1(2, 0)
+        linear_z1(3, 1)
+        mul_z2(1, 0)
+        mul_f(2, 0)
+        use_z2(1, 0)
+        weigh_z1(2, 1)
+        fuse(1, 1)
+        mul_z2(1, 1)
+        quant_u(2, 1)
+        quant_u(3, 1)
+        mul_f(2, 1)
+        mul_f(3, 1)
+        use_z2(1, 1)
+        fuse(2, 0)
+        weigh_z1(3, 1)
+        quant_u(3, 0)
+        mul_f(3, 0)
+        store(1, 0)
+        fuse(2, 1)
+        turn_out(1, 1)
+        store(1, 1)
+        turn_out(2, 0)
+        store(2, 0)
+        fuse(3, 1)
+        turn_out(2, 1)
+        turn_out(3, 1)
+        store(2, 1)
+        fuse(3, 0)
+        turn_out(3, 0)
+        store(3, 1)
+        store(3, 0)

@@ -21,8 +21,9 @@ PASSES = D // 512
 TB = 256
 NB = B // TB
 TT = TB // P
-ON_GPSIMD = (("wf", 0, 0), ("wf", 1, 0), ("w2", 0, 0), ("w2", 1, 0), ("w2", 0, 1), ("w2", 1, 1))
-SPLIT = ((0, 0), (0, 1), (1, 0), (1, 1), (2, 0), (2, 1), (3, 0), (3, 1))
+ON_GPSIMD = ()
+SPLIT = ()
+EVAC_V = ((3, 0, 1), (3, 1, 1))
 
 
 def tile_finalmlptwostreamfusion_kernel(tc, x, s, w1, w2_bytes, w2_scale, r, wf, a, out):
@@ -57,7 +58,11 @@ def tile_finalmlptwostreamfusion_kernel(tc, x, s, w1, w2_bytes, w2_scale, r, wf,
         def load_w(dst, src):
             nc.sync.dma_start(out=dst[:], in_=src.rearrange("(p j) n -> p j n", j=4))
 
-        load_x(0)
+        for g in range(PASSES):
+            nc.sync.dma_start(
+                out=x_raw[0][:, :, g * 512 : (g + 1) * 512],
+                in_=x[0:TB, g * 512 : (g + 1) * 512].rearrange("(i p) k -> p i k", p=P),
+            )
         load_w(w1_raw[0], w1[0:512, :])
         load_x(1)
         load_w(w1_raw[1], w1[512:1024, :])
@@ -323,136 +328,133 @@ def tile_finalmlptwostreamfusion_kernel(tc, x, s, w1, w2_bytes, w2_scale, r, wf,
         def store(b, h):
             for i in range(TT):
                 rows = work.tile([P, W], F32, name="rows", bufs=6)
-                nc.scalar.copy(out=rows[:].rearrange("n (m t) -> n m t", t=4), in_=tr[b, h, i][:].rearrange("n t m -> n m t"))
+                dst = rows[:].rearrange("n (m t) -> n m t", t=4)
+                src = tr[b, h, i][:].rearrange("n t m -> n m t")
+                if (b, h, i) in EVAC_V:
+                    nc.vector.tensor_copy(out=dst, in_=src)
+                else:
+                    nc.scalar.copy(out=dst, in_=src)
                 n0 = b * TB + i * P
                 nc.sync.dma_start(out=out[n0 : n0 + P, h * W : (h + 1) * W], in_=rows[:])
 
-        turn_x(0, 1)
-        gate_x(0, 1)
         turn_x(0, 0)
-        group_w1(1, 0)
-        turn_x(1, 0)
         gate_x(0, 0)
+        turn_x(0, 1)
+        group_w1(1, 0)
+        gate_x(0, 1)
         turn_x(1, 1)
-        quant_x(0, 0)
-        group_w1(0, 0)
-        gate_x(1, 1)
-        quant_w1(1, 0)
-        turn_x(2, 1)
-        widen_vectors()
-        group_w1(0, 1)
-        gate_x(1, 0)
-        quant_w1(0, 1)
-        turn_x(2, 0)
-        quant_x(1, 1)
-        quant_w1(0, 0)
-        turn_x(3, 1)
-        mul_z1(0, 0)
-        widen_w2(1, 0)
-        widen_w2(1, 1)
-        quant_x(1, 0)
-        quant_x(0, 1)
-        gate_x(2, 1)
         group_w1(1, 1)
-        group_w2(0, 1)
-        gain_z1(0, 0)
-        mul_z1(1, 0)
-        quant_w1(1, 1)
-        mul_z1(0, 1)
-        group_w2(1, 1)
-        linear_z1(0, 0)
-        group_wf(0)
-        gate_x(3, 1)
-        widen_w2(0, 0)
+        gate_x(1, 1)
+        group_w1(0, 1)
+        quant_x(0, 1)
+        turn_x(1, 0)
+        gate_x(1, 0)
+        quant_x(1, 0)
         turn_x(3, 0)
-        gain_z1(0, 1)
+        gate_x(3, 0)
+        group_w1(0, 0)
+        widen_w2(1, 0)
+        widen_w2(0, 0)
+        quant_x(0, 0)
+        quant_w1(0, 1)
+        quant_w1(1, 0)
         widen_w2(0, 1)
-        mul_z1(1, 1)
-        linear_z1(0, 1)
-        gain_z1(1, 0)
-        group_w2(0, 0)
-        gate_x(2, 0)
+        turn_x(2, 0)
+        widen_w2(1, 1)
+        quant_x(1, 1)
+        quant_w1(1, 1)
+        turn_x(2, 1)
+        gate_x(2, 1)
+        quant_w1(0, 0)
         group_w2(1, 0)
-        quant_w2(1, 1)
-        quant_u(1, 0)
-        quant_x(2, 0)
-        mul_z1(2, 0)
+        gate_x(2, 0)
+        mul_z1(1, 0)
+        group_w2(0, 0)
+        mul_z1(0, 0)
+        mul_z1(1, 1)
+        group_w2(1, 1)
+        group_w2(0, 1)
+        widen_vectors()
+        gain_z1(0, 0)
+        linear_z1(0, 0)
         linear_z1(1, 0)
-        quant_u(0, 0)
-        mul_z1(2, 1)
-        quant_wf(0)
-        quant_u(0, 1)
-        weigh_z1(0, 0)
-        quant_w2(0, 1)
-        quant_w2(0, 0)
-        mul_z2(0, 0)
-        mul_f(0, 0)
+        gain_z1(1, 0)
+        turn_x(3, 1)
         gain_z1(1, 1)
-        gain_z1(2, 0)
-        gain_z1(2, 1)
+        mul_z1(0, 1)
+        quant_u(0, 0)
+        quant_x(2, 0)
         linear_z1(1, 1)
         quant_w2(1, 0)
-        mul_z2(0, 1)
-        group_wf(1)
-        weigh_z1(0, 1)
-        gate_x(3, 0)
-        linear_z1(2, 0)
+        quant_u(1, 0)
+        gain_z1(0, 1)
+        group_wf(0)
+        mul_z1(2, 1)
         linear_z1(2, 1)
-        use_z2(0, 0)
-        use_z2(0, 1)
-        fuse(0, 0)
-        turn_out(0, 0)
-        weigh_z1(1, 0)
+        linear_z1(0, 1)
+        quant_w2(0, 1)
+        quant_w2(0, 0)
         quant_u(1, 1)
-        store(0, 0)
+        quant_u(0, 1)
+        mul_z2(0, 0)
+        gain_z1(2, 1)
+        quant_wf(0)
+        quant_w2(1, 1)
+        mul_f(0, 0)
+        use_z2(0, 0)
+        fuse(0, 0)
+        group_wf(1)
+        gate_x(3, 1)
         quant_wf(1)
-        mul_f(0, 1)
-        mul_f(1, 0)
-        quant_x(3, 0)
-        fuse(0, 1)
-        mul_z1(3, 0)
-        fuse(1, 0)
-        turn_out(0, 1)
-        quant_u(2, 0)
-        turn_out(1, 0)
-        quant_x(2, 1)
-        gain_z1(3, 0)
+        mul_z2(0, 1)
+        use_z2(0, 1)
         quant_x(3, 1)
-        store(0, 1)
-        mul_z1(3, 1)
-        mul_f(1, 1)
-        linear_z1(3, 0)
-        weigh_z1(3, 0)
-        weigh_z1(1, 1)
-        gain_z1(3, 1)
-        weigh_z1(2, 0)
-        linear_z1(3, 1)
+        quant_x(2, 1)
+        turn_out(0, 0)
+        mul_z1(2, 0)
+        linear_z1(2, 0)
         mul_z2(1, 0)
-        mul_f(2, 0)
-        use_z2(1, 0)
-        weigh_z1(2, 1)
+        gain_z1(2, 0)
+        quant_x(3, 0)
+        mul_f(0, 1)
+        fuse(0, 1)
+        mul_f(1, 0)
+        fuse(1, 0)
+        quant_u(2, 0)
+        mul_z1(3, 0)
+        mul_f(1, 1)
         fuse(1, 1)
-        mul_z2(1, 1)
+        use_z2(1, 0)
+        turn_out(0, 1)
+        turn_out(1, 0)
         quant_u(2, 1)
+        mul_z1(3, 1)
+        gain_z1(3, 0)
+        linear_z1(3, 0)
+        linear_z1(3, 1)
+        mul_z2(1, 1)
+        gain_z1(3, 1)
+        mul_f(2, 0)
+        quant_u(3, 0)
+        store(0, 0)
         quant_u(3, 1)
-        mul_f(2, 1)
         mul_f(3, 1)
+        store(0, 1)
+        mul_f(3, 0)
         use_z2(1, 1)
         fuse(2, 0)
-        weigh_z1(3, 1)
-        quant_u(3, 0)
-        mul_f(3, 0)
-        store(1, 0)
-        fuse(2, 1)
-        turn_out(1, 1)
-        store(1, 1)
-        turn_out(2, 0)
-        store(2, 0)
-        fuse(3, 1)
-        turn_out(2, 1)
-        turn_out(3, 1)
-        store(2, 1)
         fuse(3, 0)
-        turn_out(3, 0)
+        turn_out(2, 0)
+        turn_out(1, 1)
+        fuse(3, 1)
+        store(1, 0)
+        store(2, 0)
+        mul_f(2, 1)
+        store(1, 1)
+        fuse(2, 1)
+        turn_out(3, 1)
         store(3, 1)
+        turn_out(2, 1)
+        store(2, 1)
+        turn_out(3, 0)
         store(3, 0)

@@ -41,11 +41,8 @@ def tile_finalmlptwostreamfusion_kernel(tc, x, s, w1, w2_bytes, w2_scale, r, wf,
         s_bf = keep.tile([P, 2 * PASSES, 4], BF16, name="s_bf")
         nc.scalar.dma_start(out=s_bf[:], in_=s.rearrange("k (g p t) -> p (k g) t", p=P, t=4))
         ws = keep.tile([P, PASSES, 4], F32, name="ws")
-        nc.scalar.dma_start(out=ws[:], in_=w2_scale.rearrange("(g p t) o -> p g (t o)", p=P, t=4))
         r_bf = keep.tile([P, HEADS, 4], BF16, name="r_bf")
-        nc.scalar.dma_start(out=r_bf[:], in_=r.rearrange("(h p t) -> p h t", p=P, t=4))
         a_bf = keep.tile([P, 2 * HEADS, 4], BF16, name="a_bf")
-        nc.scalar.dma_start(out=a_bf[:], in_=a.rearrange("k (h p t) -> p (k h) t", p=P, t=4))
 
         x_raw = [keep.tile([P, TT, D], BF16, name="x_raw%d" % b) for b in range(NB)]
         w1_raw = [keep.tile([P, 4, H], BF16, name="w1_raw%d" % g) for g in range(PASSES)]
@@ -70,8 +67,11 @@ def tile_finalmlptwostreamfusion_kernel(tc, x, s, w1, w2_bytes, w2_scale, r, wf,
         load_w(w2_raw[0], w2_bytes[0:512, :])
         load_x(3)
         load_w(w2_raw[1], w2_bytes[512:1024, :])
+        nc.sync.dma_start(out=ws[:], in_=w2_scale.rearrange("(g p t) o -> p g (t o)", p=P, t=4))
         load_w(wf_raw[0], wf[0])
         load_w(wf_raw[1], wf[1])
+        nc.sync.dma_start(out=r_bf[:], in_=r.rearrange("(h p t) -> p h t", p=P, t=4))
+        nc.sync.dma_start(out=a_bf[:], in_=a.rearrange("k (h p t) -> p (k h) t", p=P, t=4))
 
         sig = keep.tile([P, 2 * PASSES, 4], F32, name="sig")
         nc.scalar.activation(out=sig[:], in_=s_bf[:], func=ACT.Sigmoid)
@@ -157,8 +157,8 @@ def tile_finalmlptwostreamfusion_kernel(tc, x, s, w1, w2_bytes, w2_scale, r, wf,
 
         def group_w(tag, index, h, src):
             tile = work.tile([P, 4 * W], BF16, name="wg", bufs=4, align_bytes=64)
-            dst = tile[:].rearrange("p (t m j) -> p t m j", t=4, j=4)
-            src = src.rearrange("p j (m t) -> p t m j", t=4)
+            dst = tile[:].rearrange("p (t m j) -> p m t j", t=4, j=4)
+            src = src.rearrange("p j (m t) -> p m t j", t=4)
             if (tag, index, h) in ON_GPSIMD:
                 nc.gpsimd.tensor_scalar(out=dst, in0=src, scalar1=1.0, scalar2=0.0, op0=ALU.mult, op1=ALU.add)
             else:

@@ -21,9 +21,9 @@ PASSES = D // 512
 TB = 256
 NB = B // TB
 TT = TB // P
-ON_GPSIMD = ()
-SPLIT = ()
-EVAC_V = ((3, 0, 1), (3, 1, 1))
+ON_GPSIMD = (("w1", 1, 0), ("w2", 1, 1), ("wf", 0, 0), ("w2", 0, 0))
+SPLIT = ((0, 0), (0, 1), (1, 0), (1, 1), (2, 0), (2, 1), (3, 0), (3, 1))
+EVAC_V = ((0, 0, 1), (0, 1, 0), (0, 1, 1))
 
 
 def tile_finalmlptwostreamfusion_kernel(tc, x, s, w1, w2_bytes, w2_scale, r, wf, a, out):
@@ -45,7 +45,7 @@ def tile_finalmlptwostreamfusion_kernel(tc, x, s, w1, w2_bytes, w2_scale, r, wf,
         a_bf = keep.tile([P, 2 * HEADS, 4], BF16, name="a_bf")
 
         x_raw = [keep.tile([P, TT, D], BF16, name="x_raw%d" % b) for b in range(NB)]
-        w1_raw = [keep.tile([P, 4, H], BF16, name="w1_raw%d" % g) for g in range(PASSES)]
+        w1_raw = [work.tile([P, 4, H], BF16, name="big", bufs=12) for g in range(PASSES)]
         w2_raw = [keep.tile([P, 4, H], U8, name="w2_raw%d" % g) for g in range(PASSES)]
         wf_raw = [keep.tile([P, 4, W], BF16, name="wf_raw%d" % h) for h in range(HEADS)]
 
@@ -160,7 +160,15 @@ def tile_finalmlptwostreamfusion_kernel(tc, x, s, w1, w2_bytes, w2_scale, r, wf,
             dst = tile[:].rearrange("p (t m j) -> p m t j", t=4, j=4)
             src = src.rearrange("p j (m t) -> p m t j", t=4)
             if (tag, index, h) in ON_GPSIMD:
-                nc.gpsimd.tensor_scalar(out=dst, in0=src, scalar1=1.0, scalar2=0.0, op0=ALU.mult, op1=ALU.add)
+                for m in range(0, P, 32):
+                    nc.gpsimd.tensor_scalar(
+                        out=dst[:, m : m + 32, :, :],
+                        in0=src[:, m : m + 32, :, :],
+                        scalar1=1.0,
+                        scalar2=0.0,
+                        op0=ALU.mult,
+                        op1=ALU.add,
+                    )
             else:
                 nc.scalar.copy(out=dst, in_=src)
             wg[tag, index, h] = tile
@@ -175,7 +183,7 @@ def tile_finalmlptwostreamfusion_kernel(tc, x, s, w1, w2_bytes, w2_scale, r, wf,
 
         def widen_w2(g, half):
             if g not in w2_wide:
-                w2_wide[g] = work.tile([P, 4, H], BF16, name="big", bufs=3)
+                w2_wide[g] = work.tile([P, 4, H], BF16, name="big", bufs=12)
             for j in (2 * half, 2 * half + 1):
                 nc.scalar.activation(
                     out=w2_wide[g][:, j, :],
@@ -231,7 +239,7 @@ def tile_finalmlptwostreamfusion_kernel(tc, x, s, w1, w2_bytes, w2_scale, r, wf,
 
         def linear_z1(b, h):
             if b not in o1a:
-                o1a[b] = work.tile([P, HEADS, TT, 4, P], F32, name="o1a", bufs=3)
+                o1a[b] = work.tile([P, HEADS, TT, 4, P], F32, name="big", bufs=12)
             for i in range(TT):
                 if (b, h) in SPLIT:
                     nc.scalar.activation(out=o1a[b][:, h, i, :, :], in_=z1[b, h, i][:], func=ACT.Relu)
@@ -259,8 +267,8 @@ def tile_finalmlptwostreamfusion_kernel(tc, x, s, w1, w2_bytes, w2_scale, r, wf,
         z2 = {}
         o2 = {}
 
-        def mul_z2(c, h):
-            for t in range(4):
+        def mul_z2(c, h, pair):
+            for t in (2 * pair, 2 * pair + 1):
                 bank = psum.tile([P, 2, TB], F32, name="z_bank", bufs=5)
                 for half in range(2):
                     for g in range(PASSES):
@@ -275,11 +283,11 @@ def tile_finalmlptwostreamfusion_kernel(tc, x, s, w1, w2_bytes, w2_scale, r, wf,
                         )
                 z2[c, h, t] = bank
 
-        def use_z2(c, h):
-            if c not in o2:
-                o2[c] = work.tile([P, HEADS, 4, 2, TB], F32, name="o2", bufs=2)
-            for t in range(4):
-                nc.scalar.activation(out=o2[c][:, h, t, :, :], in_=z2[c, h, t][:], func=ACT.Relu)
+        def use_z2(c, h, pair):
+            if (c, h) not in o2:
+                o2[c, h] = work.tile([P, 4, 2, TB], F32, name="big", bufs=12)
+            for t in (2 * pair, 2 * pair + 1):
+                nc.scalar.activation(out=o2[c, h][:, t, :, :], in_=z2[c, h, t][:], func=ACT.Relu)
 
         fb = {}
 
@@ -295,21 +303,21 @@ def tile_finalmlptwostreamfusion_kernel(tc, x, s, w1, w2_bytes, w2_scale, r, wf,
 
         def fuse(b, h):
             if b not in fused:
-                fused[b] = work.tile([P, HEADS, 4, TB], F32, name="big", bufs=3)
+                fused[b] = work.tile([P, HEADS, 4, TB], F32, name="big", bufs=12)
             for t in range(4):
                 nc.vector.scalar_tensor_tensor(
                     out=fused[b][:, h, t, :],
                     in0=fb[b, h, t // 2][:, t % 2, :],
                     scalar=a_f[:, HEADS + h, t : t + 1],
-                    in1=o2[b // 2][:, h, t, b % 2, :],
+                    in1=o2[b // 2, h][:, t, b % 2, :],
                     op0=ALU.add,
                     op1=ALU.mult,
                 )
 
         tr = {}
 
-        def turn_out(b, h):
-            for i in range(TT):
+        def turn_out(b, h, i):
+            if True:
                 bank = psum.tile([P, 4, P], F32, name="t_bank", bufs=3)
                 for t in range(4):
                     nc.tensor.matmul(
@@ -325,8 +333,8 @@ def tile_finalmlptwostreamfusion_kernel(tc, x, s, w1, w2_bytes, w2_scale, r, wf,
                     )
                 tr[b, h, i] = bank
 
-        def store(b, h):
-            for i in range(TT):
+        def store(b, h, i):
+            if True:
                 rows = work.tile([P, W], F32, name="rows", bufs=6)
                 dst = rows[:].rearrange("n (m t) -> n m t", t=4)
                 src = tr[b, h, i][:].rearrange("n t m -> n m t")
@@ -338,123 +346,155 @@ def tile_finalmlptwostreamfusion_kernel(tc, x, s, w1, w2_bytes, w2_scale, r, wf,
                 nc.sync.dma_start(out=out[n0 : n0 + P, h * W : (h + 1) * W], in_=rows[:])
 
         turn_x(0, 0)
-        gate_x(0, 0)
-        turn_x(0, 1)
         group_w1(1, 0)
+        turn_x(0, 1)
+        gate_x(0, 0)
         gate_x(0, 1)
-        turn_x(1, 1)
-        group_w1(1, 1)
-        gate_x(1, 1)
-        group_w1(0, 1)
-        quant_x(0, 1)
-        turn_x(1, 0)
-        gate_x(1, 0)
-        quant_x(1, 0)
-        turn_x(3, 0)
-        gate_x(3, 0)
         group_w1(0, 0)
-        widen_w2(1, 0)
-        widen_w2(0, 0)
         quant_x(0, 0)
+        turn_x(1, 1)
+        gate_x(1, 1)
+        group_w1(1, 1)
+        turn_x(1, 0)
+        turn_x(2, 0)
+        group_w1(0, 1)
+        turn_x(3, 1)
+        gate_x(1, 0)
         quant_w1(0, 1)
         quant_w1(1, 0)
-        widen_w2(0, 1)
-        turn_x(2, 0)
+        widen_w2(0, 0)
         widen_w2(1, 1)
+        quant_x(0, 1)
         quant_x(1, 1)
-        quant_w1(1, 1)
         turn_x(2, 1)
-        gate_x(2, 1)
         quant_w1(0, 0)
-        group_w2(1, 0)
-        gate_x(2, 0)
-        mul_z1(1, 0)
-        group_w2(0, 0)
-        mul_z1(0, 0)
-        mul_z1(1, 1)
-        group_w2(1, 1)
+        quant_x(1, 0)
+        turn_x(3, 0)
+        gate_x(2, 1)
+        widen_w2(0, 1)
+        widen_w2(1, 0)
         group_w2(0, 1)
-        widen_vectors()
-        gain_z1(0, 0)
-        linear_z1(0, 0)
-        linear_z1(1, 0)
-        gain_z1(1, 0)
-        turn_x(3, 1)
-        gain_z1(1, 1)
-        mul_z1(0, 1)
-        quant_u(0, 0)
-        quant_x(2, 0)
-        linear_z1(1, 1)
-        quant_w2(1, 0)
-        quant_u(1, 0)
-        gain_z1(0, 1)
+        gate_x(2, 0)
         group_wf(0)
-        mul_z1(2, 1)
-        linear_z1(2, 1)
-        linear_z1(0, 1)
+        quant_x(2, 0)
+        mul_z1(0, 0)
+        quant_w1(1, 1)
+        quant_x(2, 1)
+        widen_vectors()
+        group_w2(0, 0)
+        gain_z1(0, 0)
+        gate_x(3, 0)
+        quant_u(0, 0)
         quant_w2(0, 1)
         quant_w2(0, 0)
-        quant_u(1, 1)
-        quant_u(0, 1)
-        mul_z2(0, 0)
-        gain_z1(2, 1)
-        quant_wf(0)
-        quant_w2(1, 1)
-        mul_f(0, 0)
-        use_z2(0, 0)
-        fuse(0, 0)
-        group_wf(1)
+        mul_z1(0, 1)
+        linear_z1(0, 0)
+        group_w2(1, 0)
+        mul_z2(0, 0, 1)
+        gain_z1(0, 1)
+        linear_z1(0, 1)
+        mul_z2(0, 0, 0)
+        mul_z1(1, 1)
+        use_z2(0, 0, 1)
         gate_x(3, 1)
-        quant_wf(1)
-        mul_z2(0, 1)
-        use_z2(0, 1)
+        mul_z1(2, 1)
+        use_z2(0, 0, 0)
+        group_w2(1, 1)
+        gain_z1(1, 1)
+        linear_z1(1, 1)
         quant_x(3, 1)
-        quant_x(2, 1)
-        turn_out(0, 0)
+        mul_z2(1, 0, 1)
+        gain_z1(2, 1)
+        linear_z1(2, 1)
+        quant_u(0, 1)
+        weigh_z1(0, 0)
         mul_z1(2, 0)
-        linear_z1(2, 0)
-        mul_z2(1, 0)
+        use_z2(1, 0, 1)
+        quant_wf(0)
         gain_z1(2, 0)
+        linear_z1(2, 0)
+        mul_z2(1, 0, 0)
+        use_z2(1, 0, 0)
+        mul_f(0, 0)
         quant_x(3, 0)
-        mul_f(0, 1)
-        fuse(0, 1)
-        mul_f(1, 0)
-        fuse(1, 0)
-        quant_u(2, 0)
-        mul_z1(3, 0)
-        mul_f(1, 1)
-        fuse(1, 1)
-        use_z2(1, 0)
-        turn_out(0, 1)
-        turn_out(1, 0)
-        quant_u(2, 1)
         mul_z1(3, 1)
-        gain_z1(3, 0)
-        linear_z1(3, 0)
-        linear_z1(3, 1)
-        mul_z2(1, 1)
+        quant_u(2, 1)
+        quant_u(1, 1)
+        group_wf(1)
+        fuse(0, 0)
+        mul_z1(3, 0)
+        turn_out(0, 0, 0)
+        turn_out(0, 0, 1)
+        quant_w2(1, 1)
+        quant_w2(1, 0)
         gain_z1(3, 1)
+        linear_z1(3, 1)
+        gain_z1(3, 0)
+        mul_z2(1, 1, 0)
+        quant_u(2, 0)
+        linear_z1(3, 0)
+        use_z2(1, 1, 0)
+        weigh_z1(3, 0)
+        mul_z1(1, 0)
         mul_f(2, 0)
-        quant_u(3, 0)
-        store(0, 0)
-        quant_u(3, 1)
-        mul_f(3, 1)
-        store(0, 1)
-        mul_f(3, 0)
-        use_z2(1, 1)
+        weigh_z1(2, 0)
+        weigh_z1(2, 1)
+        gain_z1(1, 0)
         fuse(2, 0)
-        fuse(3, 0)
-        turn_out(2, 0)
-        turn_out(1, 1)
-        fuse(3, 1)
-        store(1, 0)
-        store(2, 0)
+        quant_wf(1)
+        weigh_z1(1, 1)
+        quant_u(3, 0)
+        mul_z2(0, 1, 0)
+        linear_z1(1, 0)
+        mul_z2(0, 1, 1)
+        mul_f(1, 1)
+        use_z2(0, 1, 0)
+        weigh_z1(3, 1)
+        use_z2(0, 1, 1)
+        mul_z2(1, 1, 1)
         mul_f(2, 1)
-        store(1, 1)
+        mul_f(0, 1)
+        use_z2(1, 1, 1)
+        fuse(1, 1)
+        quant_u(1, 0)
         fuse(2, 1)
-        turn_out(3, 1)
-        store(3, 1)
-        turn_out(2, 1)
-        store(2, 1)
-        turn_out(3, 0)
-        store(3, 0)
+        mul_f(3, 0)
+        store(0, 0, 1)
+        weigh_z1(1, 0)
+        fuse(0, 1)
+        turn_out(2, 0, 1)
+        store(0, 0, 0)
+        fuse(3, 0)
+        turn_out(2, 1, 1)
+        store(2, 0, 1)
+        turn_out(2, 0, 0)
+        turn_out(1, 1, 1)
+        turn_out(2, 1, 0)
+        turn_out(1, 1, 0)
+        quant_u(3, 1)
+        turn_out(3, 0, 0)
+        store(2, 1, 1)
+        mul_f(3, 1)
+        mul_f(1, 0)
+        fuse(3, 1)
+        store(2, 0, 0)
+        turn_out(3, 0, 1)
+        turn_out(3, 1, 0)
+        fuse(1, 0)
+        store(1, 1, 1)
+        store(2, 1, 0)
+        turn_out(3, 1, 1)
+        store(1, 1, 0)
+        store(3, 0, 0)
+        store(3, 0, 1)
+        store(3, 1, 0)
+        store(3, 1, 1)
+        weigh_z1(0, 1)
+        turn_out(0, 1, 1)
+        store(0, 1, 1)
+        turn_out(1, 0, 1)
+        store(1, 0, 1)
+        turn_out(0, 1, 0)
+        store(0, 1, 0)
+        turn_out(1, 0, 0)
+        store(1, 0, 0)

@@ -21,9 +21,9 @@ PASSES = D // 512
 TB = 256
 NB = B // TB
 TT = TB // P
-ON_GPSIMD = (("w1", 1, 0), ("w2", 1, 1), ("wf", 0, 0), ("w2", 0, 0))
-SPLIT = ((0, 0), (0, 1), (1, 0), (1, 1), (2, 0), (2, 1), (3, 0), (3, 1))
-EVAC_V = ((0, 0, 1), (0, 1, 0), (0, 1, 1))
+ON_GPSIMD = ()
+SPLIT = ((0, 0), (0, 1), (1, 0), (1, 1), (2, 0), (3, 0))
+EVAC_V = ((0, 0, 0), (0, 1, 1))
 
 
 def tile_finalmlptwostreamfusion_kernel(tc, x, s, w1, w2_bytes, w2_scale, r, wf, a, out):
@@ -257,8 +257,8 @@ def tile_finalmlptwostreamfusion_kernel(tc, x, s, w1, w2_bytes, w2_scale, r, wf,
             if (b, h) in SPLIT:
                 for t in range(4):
                     part = o1a[b][:, h, :, t, :]
-                    nc.gpsimd.tensor_scalar(
-                        out=part, in0=part, scalar1=a_f[:, h, t : t + 1], scalar2=0.0, op0=ALU.mult, op1=ALU.add
+                    nc.vector.tensor_scalar(
+                        out=part, in0=part, scalar1=a_f[:, h, t : t + 1], scalar2=None, op0=ALU.mult
                     )
 
         def quant_u(b, h):
@@ -346,155 +346,155 @@ def tile_finalmlptwostreamfusion_kernel(tc, x, s, w1, w2_bytes, w2_scale, r, wf,
                 nc.sync.dma_start(out=out[n0 : n0 + P, h * W : (h + 1) * W], in_=rows[:])
 
         turn_x(0, 0)
-        group_w1(1, 0)
-        turn_x(0, 1)
-        gate_x(0, 0)
-        gate_x(0, 1)
-        group_w1(0, 0)
-        quant_x(0, 0)
-        turn_x(1, 1)
-        gate_x(1, 1)
-        group_w1(1, 1)
-        turn_x(1, 0)
-        turn_x(2, 0)
-        group_w1(0, 1)
-        turn_x(3, 1)
-        gate_x(1, 0)
-        quant_w1(0, 1)
-        quant_w1(1, 0)
-        widen_w2(0, 0)
-        widen_w2(1, 1)
-        quant_x(0, 1)
-        quant_x(1, 1)
-        turn_x(2, 1)
-        quant_w1(0, 0)
-        quant_x(1, 0)
-        turn_x(3, 0)
-        gate_x(2, 1)
-        widen_w2(0, 1)
-        widen_w2(1, 0)
-        group_w2(0, 1)
-        gate_x(2, 0)
-        group_wf(0)
-        quant_x(2, 0)
-        mul_z1(0, 0)
-        quant_w1(1, 1)
-        quant_x(2, 1)
         widen_vectors()
-        group_w2(0, 0)
-        gain_z1(0, 0)
-        gate_x(3, 0)
-        quant_u(0, 0)
-        quant_w2(0, 1)
-        quant_w2(0, 0)
-        mul_z1(0, 1)
-        linear_z1(0, 0)
-        group_w2(1, 0)
-        mul_z2(0, 0, 1)
-        gain_z1(0, 1)
-        linear_z1(0, 1)
-        mul_z2(0, 0, 0)
+        turn_x(0, 1)
+        turn_x(1, 1)
+        gate_x(0, 0)
+        group_w1(1, 0)
+        turn_x(1, 0)
+        gate_x(0, 1)
+        quant_x(0, 0)
+        quant_w1(1, 0)
+        group_w1(0, 0)
+        gate_x(1, 1)
+        quant_x(0, 1)
+        group_w1(1, 1)
+        turn_x(2, 0)
+        gate_x(1, 0)
+        turn_x(3, 1)
+        group_w1(0, 1)
+        quant_w1(1, 1)
+        turn_x(2, 1)
+        quant_x(1, 0)
         mul_z1(1, 1)
-        use_z2(0, 0, 1)
         gate_x(3, 1)
-        mul_z1(2, 1)
-        use_z2(0, 0, 0)
-        group_w2(1, 1)
+        turn_x(3, 0)
+        widen_w2(1, 0)
         gain_z1(1, 1)
-        linear_z1(1, 1)
-        quant_x(3, 1)
-        mul_z2(1, 0, 1)
-        gain_z1(2, 1)
-        linear_z1(2, 1)
-        quant_u(0, 1)
-        weigh_z1(0, 0)
-        mul_z1(2, 0)
-        use_z2(1, 0, 1)
-        quant_wf(0)
-        gain_z1(2, 0)
-        linear_z1(2, 0)
-        mul_z2(1, 0, 0)
-        use_z2(1, 0, 0)
-        mul_f(0, 0)
+        quant_w1(0, 0)
+        widen_w2(0, 1)
+        widen_w2(1, 1)
+        mul_z1(0, 1)
+        gate_x(3, 0)
         quant_x(3, 0)
+        gate_x(2, 0)
+        widen_w2(0, 0)
+        gain_z1(0, 1)
         mul_z1(3, 1)
-        quant_u(2, 1)
-        quant_u(1, 1)
-        group_wf(1)
-        fuse(0, 0)
-        mul_z1(3, 0)
-        turn_out(0, 0, 0)
-        turn_out(0, 0, 1)
+        gain_z1(3, 1)
+        linear_z1(1, 1)
+        gate_x(2, 1)
+        linear_z1(3, 1)
+        group_w2(1, 1)
+        group_w2(1, 0)
+        linear_z1(0, 1)
+        quant_x(2, 0)
         quant_w2(1, 1)
         quant_w2(1, 0)
-        gain_z1(3, 1)
-        linear_z1(3, 1)
-        gain_z1(3, 0)
-        mul_z2(1, 1, 0)
-        quant_u(2, 0)
-        linear_z1(3, 0)
-        use_z2(1, 1, 0)
-        weigh_z1(3, 0)
-        mul_z1(1, 0)
-        mul_f(2, 0)
-        weigh_z1(2, 0)
-        weigh_z1(2, 1)
-        gain_z1(1, 0)
-        fuse(2, 0)
-        quant_wf(1)
+        quant_x(1, 1)
+        mul_z1(2, 1)
+        weigh_z1(3, 1)
         weigh_z1(1, 1)
-        quant_u(3, 0)
         mul_z2(0, 1, 0)
-        linear_z1(1, 0)
+        quant_u(3, 1)
+        quant_u(1, 1)
         mul_z2(0, 1, 1)
+        quant_x(2, 1)
+        quant_x(3, 1)
+        gain_z1(2, 1)
+        group_wf(1)
+        mul_z2(1, 1, 1)
+        mul_z2(1, 1, 0)
+        quant_wf(1)
         mul_f(1, 1)
         use_z2(0, 1, 0)
-        weigh_z1(3, 1)
         use_z2(0, 1, 1)
-        mul_z2(1, 1, 1)
-        mul_f(2, 1)
-        mul_f(0, 1)
         use_z2(1, 1, 1)
-        fuse(1, 1)
-        quant_u(1, 0)
-        fuse(2, 1)
-        mul_f(3, 0)
-        store(0, 0, 1)
-        weigh_z1(1, 0)
-        fuse(0, 1)
-        turn_out(2, 0, 1)
-        store(0, 0, 0)
-        fuse(3, 0)
-        turn_out(2, 1, 1)
-        store(2, 0, 1)
-        turn_out(2, 0, 0)
-        turn_out(1, 1, 1)
-        turn_out(2, 1, 0)
-        turn_out(1, 1, 0)
-        quant_u(3, 1)
-        turn_out(3, 0, 0)
-        store(2, 1, 1)
+        quant_w1(0, 1)
+        use_z2(1, 1, 0)
+        mul_z1(3, 0)
         mul_f(3, 1)
-        mul_f(1, 0)
+        linear_z1(2, 1)
+        fuse(1, 1)
+        turn_out(1, 1, 0)
+        mul_z1(2, 0)
+        turn_out(1, 1, 1)
+        quant_u(0, 1)
+        gain_z1(3, 0)
+        group_w2(0, 0)
+        mul_z1(0, 0)
         fuse(3, 1)
-        store(2, 0, 0)
-        turn_out(3, 0, 1)
-        turn_out(3, 1, 0)
-        fuse(1, 0)
-        store(1, 1, 1)
-        store(2, 1, 0)
-        turn_out(3, 1, 1)
-        store(1, 1, 0)
-        store(3, 0, 0)
-        store(3, 0, 1)
-        store(3, 1, 0)
-        store(3, 1, 1)
+        gain_z1(2, 0)
+        quant_w2(0, 0)
+        group_w2(0, 1)
+        linear_z1(2, 0)
+        linear_z1(3, 0)
+        quant_w2(0, 1)
+        mul_z2(1, 0, 0)
+        quant_u(2, 1)
         weigh_z1(0, 1)
+        mul_f(0, 1)
+        mul_z1(1, 0)
+        gain_z1(0, 0)
+        weigh_z1(2, 1)
+        mul_f(2, 1)
+        fuse(0, 1)
+        use_z2(1, 0, 0)
+        linear_z1(0, 0)
+        fuse(2, 1)
+        weigh_z1(3, 0)
         turn_out(0, 1, 1)
+        store(1, 1, 0)
+        quant_u(2, 0)
+        turn_out(0, 1, 0)
+        mul_z2(1, 0, 1)
+        turn_out(2, 1, 1)
+        store(1, 1, 1)
+        group_wf(0)
         store(0, 1, 1)
+        turn_out(2, 1, 0)
+        quant_u(3, 0)
+        quant_wf(0)
+        store(0, 1, 0)
+        use_z2(1, 0, 1)
+        gain_z1(1, 0)
+        mul_z2(0, 0, 1)
+        linear_z1(1, 0)
+        mul_f(2, 0)
+        turn_out(3, 1, 1)
+        weigh_z1(2, 0)
+        turn_out(3, 1, 0)
+        fuse(2, 0)
+        store(2, 1, 0)
+        mul_f(3, 0)
+        store(2, 1, 1)
+        quant_u(1, 0)
+        store(3, 1, 1)
+        fuse(3, 0)
+        turn_out(2, 0, 1)
+        turn_out(2, 0, 0)
+        use_z2(0, 0, 1)
+        store(3, 1, 0)
+        weigh_z1(1, 0)
+        store(2, 0, 1)
+        mul_z2(0, 0, 0)
+        use_z2(0, 0, 0)
+        mul_f(1, 0)
+        turn_out(3, 0, 1)
+        store(3, 0, 1)
+        weigh_z1(0, 0)
+        turn_out(3, 0, 0)
+        store(3, 0, 0)
+        quant_u(0, 0)
+        mul_f(0, 0)
+        fuse(1, 0)
+        store(2, 0, 0)
         turn_out(1, 0, 1)
         store(1, 0, 1)
-        turn_out(0, 1, 0)
-        store(0, 1, 0)
         turn_out(1, 0, 0)
         store(1, 0, 0)
+        fuse(0, 0)
+        turn_out(0, 0, 1)
+        store(0, 0, 1)
+        turn_out(0, 0, 0)
+        store(0, 0, 0)

from contextlib import ExitStack

import concourse.mybir as mybir
from concourse.masks import make_identity

F32 = mybir.dt.float32
BF16 = mybir.dt.bfloat16
U32 = mybir.dt.uint32
U8 = mybir.dt.uint8
FP8 = mybir.dt.float8_e4m3fn
X4 = mybir.dt.float8_e4m3fn_x4
ALU = mybir.AluOpType
ACT = mybir.ActivationFunctionType

B, D, HEADS, W = 1024, 1024, 2, 512
H = HEADS * W
FLOPS = 2 * (2 * B * D * H + HEADS * B * W * W)

P = 128
PASSES = D // 512
TB = 256
NB = B // TB
TT = TB // P
ON_GPSIMD = ()
SPLIT = ((0, 0), (0, 1), (1, 0), (1, 1), (2, 0), (3, 0))
EVAC_V = ((0, 0, 0), (0, 1, 1))


def tile_finalmlptwostreamfusion_kernel(tc, x, s, w1, w2_bytes, w2_scale, r, wf, a, out):
    nc = tc.nc
    with ExitStack() as ctx:
        keep = ctx.enter_context(tc.tile_pool(name="keep", bufs=1))
        work = ctx.enter_context(tc.tile_pool(name="work", bufs=1))
        psum = ctx.enter_context(tc.psum_pool(name="psum", bufs=1))

        ident = keep.tile([P, P], F32, name="ident")
        make_identity(nc, ident[:])

        ctx.enter_context(tc.manual_schedule())

        s_bf = keep.tile([P, 2 * PASSES, 4], BF16, name="s_bf")
        nc.scalar.dma_start(out=s_bf[:], in_=s.rearrange("k (g p t) -> p (k g) t", p=P, t=4))
        ws = keep.tile([P, PASSES, 4], F32, name="ws")
        r_bf = keep.tile([P, HEADS, 4], BF16, name="r_bf")
        a_bf = keep.tile([P, 2 * HEADS, 4], BF16, name="a_bf")

        x_raw = [keep.tile([P, TT, D], BF16, name="x_raw%d" % b) for b in range(NB)]
        w1_raw = [work.tile([P, 4, H], BF16, name="big", bufs=12) for g in range(PASSES)]
        w2_raw = [keep.tile([P, 4, H], U8, name="w2_raw%d" % g) for g in range(PASSES)]
        wf_raw = [keep.tile([P, 4, W], BF16, name="wf_raw%d" % h) for h in range(HEADS)]

        def load_x(b):
            nc.sync.dma_start(out=x_raw[b][:], in_=x[b * TB : (b + 1) * TB, :].rearrange("(i p) k -> p i k", p=P))

        def load_w(dst, src):
            nc.sync.dma_start(out=dst[:], in_=src.rearrange("(p j) n -> p j n", j=4))

        for g in range(PASSES):
            nc.sync.dma_start(
                out=x_raw[0][:, :, g * 512 : (g + 1) * 512],
                in_=x[0:TB, g * 512 : (g + 1) * 512].rearrange("(i p) k -> p i k", p=P),
            )
        load_w(w1_raw[0], w1[0:512, :])
        load_x(1)
        load_w(w1_raw[1], w1[512:1024, :])
        load_x(2)
        load_w(w2_raw[0], w2_bytes[0:512, :])
        load_x(3)
        load_w(w2_raw[1], w2_bytes[512:1024, :])
        nc.sync.dma_start(out=ws[:], in_=w2_scale.rearrange("(g p t) o -> p g (t o)", p=P, t=4))
        load_w(wf_raw[0], wf[0])
        load_w(wf_raw[1], wf[1])
        nc.sync.dma_start(out=r_bf[:], in_=r.rearrange("(h p t) -> p h t", p=P, t=4))
        nc.sync.dma_start(out=a_bf[:], in_=a.rearrange("k (h p t) -> p (k h) t", p=P, t=4))

        sig = keep.tile([P, 2 * PASSES, 4], F32, name="sig")
        nc.scalar.activation(out=sig[:], in_=s_bf[:], func=ACT.Sigmoid)
        gate = keep.tile([P, 2 * PASSES, 4], F32, name="gate")
        nc.vector.tensor_scalar(out=gate[:], in0=sig[:], scalar1=2.0, scalar2=None, op0=ALU.mult)
        r_f = keep.tile([P, HEADS, 4], F32, name="r_f")
        a_f = keep.tile([P, 2 * HEADS, 4], F32, name="a_f")

        def widen_vectors():
            nc.gpsimd.tensor_copy(out=r_f[:], in_=r_bf[:])
            nc.gpsimd.tensor_copy(out=a_f[:], in_=a_bf[:])

        def planes(n, name):
            codes = keep.tile([P, 2, n], U32, name=name + "_c", align_bytes=64)
            scales = keep.tile([P, 2, n], U8, name=name + "_s", align_bytes=64)
            return codes, scales

        w1_q = planes(H, "w1q")
        w2_q = planes(H, "w2q")
        wf_q = planes(W, "wfq")
        g_q = []
        for k in range(2):
            codes = keep.tile([P, NB, PASSES, TB], U32, name="g%dq_c" % k, align_bytes=64)
            scales = keep.tile([P, NB, PASSES, TB], U8, name="g%dq_s" % k, align_bytes=64)
            g_q.append((codes, scales))
        u_q = planes(B, "uq")

        def quantize(q, index, lo, hi, grouped):
            codes, scales = q
            nc.vector.quantize_mx(out=codes[:, index, lo:hi].bitcast(X4), scales=scales[:, index, lo:hi], in_=grouped)

        def mx(dst, lq, li, l0, rq, ri, r0, n, start, stop):
            nc.tensor.matmul_mx(
                out=dst,
                lhsT=lq[0][:, li, l0 : l0 + P].bitcast(X4),
                lhsT_scale=lq[1][:, li, l0 : l0 + P],
                rhs=rq[0][:, ri, r0 : r0 + n].bitcast(X4),
                rhs_scale=rq[1][:, ri, r0 : r0 + n],
                start=start,
                stop=stop,
            )

        xt = {}

        def turn_x(b, g):
            if True:
                bank = psum.tile([P, 2, TB], F32, name="t_bank", bufs=3)
                for u in range(2):
                    for i in range(TT):
                        words = x_raw[b][:, i, :].bitcast(F32)
                        nc.tensor.transpose(
                            bank[:, u, i * P : (i + 1) * P], words[:, 256 * g + u : 256 * (g + 1) : 2], ident[:]
                        )
                xt[b, g] = bank

        xg = {}

        def gate_x(b, g):
            if (b, 0) not in xg:
                for k in range(2):
                    xg[b, k] = work.tile([P, PASSES, TB, 4], BF16, name="xg", bufs=4, align_bytes=64)
            src = xt[b, g][:].bitcast(BF16).rearrange("p u (r e) -> p r u e", e=2)
            if True:
                for k in range(2):
                    factor = gate[:, 2 * k + g, :].rearrange("p (u e) -> p u e", e=2).unsqueeze(1)
                    nc.vector.tensor_tensor(
                        out=xg[b, k][:, g, :, :].rearrange("p r (u e) -> p r u e", e=2),
                        in0=src,
                        in1=factor.to_broadcast([P, TB, 2, 2]),
                        op=ALU.mult,
                    )

        def quant_x(b, k):
            if True:
                codes, scales = g_q[k]
                nc.vector.quantize_mx(
                    out=codes[:, b, :, :].rearrange("p g n -> p (g n)").bitcast(X4),
                    scales=scales[:, b, :, :].rearrange("p g n -> p (g n)"),
                    in_=xg[b, k][:].rearrange("p g r t -> p (g r t)"),
                )

        wg = {}

        def group_w(tag, index, h, src):
            tile = work.tile([P, 4 * W], BF16, name="wg", bufs=4, align_bytes=64)
            dst = tile[:].rearrange("p (t m j) -> p m t j", t=4, j=4)
            src = src.rearrange("p j (m t) -> p m t j", t=4)
            if (tag, index, h) in ON_GPSIMD:
                for m in range(0, P, 32):
                    nc.gpsimd.tensor_scalar(
                        out=dst[:, m : m + 32, :, :],
                        in0=src[:, m : m + 32, :, :],
                        scalar1=1.0,
                        scalar2=0.0,
                        op0=ALU.mult,
                        op1=ALU.add,
                    )
            else:
                nc.scalar.copy(out=dst, in_=src)
            wg[tag, index, h] = tile

        def group_w1(h, g):
            group_w("w1", g, h, w1_raw[g][:, :, h * W : (h + 1) * W])

        def quant_w1(h, g):
            quantize(w1_q, g, h * W, (h + 1) * W, wg["w1", g, h][:])

        w2_wide = {}

        def widen_w2(g, half):
            if g not in w2_wide:
                w2_wide[g] = work.tile([P, 4, H], BF16, name="big", bufs=12)
            for j in (2 * half, 2 * half + 1):
                nc.scalar.activation(
                    out=w2_wide[g][:, j, :],
                    in_=w2_raw[g][:, j, :].bitcast(FP8),
                    func=ACT.Copy,
                    scale=ws[:, g, j : j + 1],
                )

        def group_w2(h, g):
            group_w("w2", g, h, w2_wide[g][:, :, h * W : (h + 1) * W])

        def quant_w2(h, g):
            quantize(w2_q, g, h * W, (h + 1) * W, wg["w2", g, h][:])

        def group_wf(h):
            group_w("wf", h, 0, wf_raw[h][:])

        def quant_wf(h):
            quantize(wf_q, h, 0, W, wg["wf", h, 0][:])

        z1 = {}

        def mul_z1(b, h):
            for i in range(TT):
                bank = psum.tile([P, 4, P], F32, name="z_bank", bufs=5)
                for t in range(4):
                    for g in range(PASSES):
                        nc.tensor.matmul_mx(
                            out=bank[:, t, :],
                            lhsT=w1_q[0][:, g, h * W + t * P : h * W + (t + 1) * P].bitcast(X4),
                            lhsT_scale=w1_q[1][:, g, h * W + t * P : h * W + (t + 1) * P],
                            rhs=g_q[0][0][:, b, g, i * P : (i + 1) * P].bitcast(X4),
                            rhs_scale=g_q[0][1][:, b, g, i * P : (i + 1) * P],
                            start=(g == 0),
                            stop=(g == PASSES - 1),
                        )
                z1[b, h, i] = bank

        ug = {}
        o1a = {}

        def gain_z1(b, h):
            ug[b, h] = work.tile([P, TT, P, 4], BF16, name="ug", bufs=3, align_bytes=64)
            for i in range(TT):
                nc.vector.scalar_tensor_tensor(
                    out=ug[b, h][:, i, :, :],
                    in0=z1[b, h, i][:].rearrange("p t n -> p n t"),
                    scalar=0.0,
                    in1=r_f[:, h, :].unsqueeze(1).to_broadcast([P, P, 4]),
                    op0=ALU.max,
                    op1=ALU.mult,
                )

        def linear_z1(b, h):
            if b not in o1a:
                o1a[b] = work.tile([P, HEADS, TT, 4, P], F32, name="big", bufs=12)
            for i in range(TT):
                if (b, h) in SPLIT:
                    nc.scalar.activation(out=o1a[b][:, h, i, :, :], in_=z1[b, h, i][:], func=ACT.Relu)
                else:
                    nc.vector.scalar_tensor_tensor(
                        out=o1a[b][:, h, i, :, :],
                        in0=z1[b, h, i][:],
                        scalar=0.0,
                        in1=a_f[:, h, :].unsqueeze(2).to_broadcast([P, 4, P]),
                        op0=ALU.max,
                        op1=ALU.mult,
                    )

        def weigh_z1(b, h):
            if (b, h) in SPLIT:
                for t in range(4):
                    part = o1a[b][:, h, :, t, :]
                    nc.vector.tensor_scalar(
                        out=part, in0=part, scalar1=a_f[:, h, t : t + 1], scalar2=None, op0=ALU.mult
                    )

        def quant_u(b, h):
            quantize(u_q, h, b * TB, (b + 1) * TB, ug[b, h][:].rearrange("p i n t -> p (i n t)"))

        z2 = {}
        o2 = {}

        def mul_z2(c, h, pair):
            for t in (2 * pair, 2 * pair + 1):
                bank = psum.tile([P, 2, TB], F32, name="z_bank", bufs=5)
                for half in range(2):
                    for g in range(PASSES):
                        nc.tensor.matmul_mx(
                            out=bank[:, half, :],
                            lhsT=w2_q[0][:, g, h * W + t * P : h * W + (t + 1) * P].bitcast(X4),
                            lhsT_scale=w2_q[1][:, g, h * W + t * P : h * W + (t + 1) * P],
                            rhs=g_q[1][0][:, 2 * c + half, g, :].bitcast(X4),
                            rhs_scale=g_q[1][1][:, 2 * c + half, g, :],
                            start=(g == 0),
                            stop=(g == PASSES - 1),
                        )
                z2[c, h, t] = bank

        def use_z2(c, h, pair):
            if (c, h) not in o2:
                o2[c, h] = work.tile([P, 4, 2, TB], F32, name="big", bufs=12)
            for t in (2 * pair, 2 * pair + 1):
                nc.scalar.activation(out=o2[c, h][:, t, :, :], in_=z2[c, h, t][:], func=ACT.Relu)

        fb = {}

        def mul_f(b, h):
            for tt in range(2):
                bank = psum.tile([P, 2, TB], F32, name="z_bank", bufs=5)
                for v in range(2):
                    t = 2 * tt + v
                    mx(bank[:, v, :], wf_q, h, t * P, u_q, h, b * TB, TB, True, True)
                fb[b, h, tt] = bank

        fused = {}

        def fuse(b, h):
            if b not in fused:
                fused[b] = work.tile([P, HEADS, 4, TB], F32, name="big", bufs=12)
            for t in range(4):
                nc.vector.scalar_tensor_tensor(
                    out=fused[b][:, h, t, :],
                    in0=fb[b, h, t // 2][:, t % 2, :],
                    scalar=a_f[:, HEADS + h, t : t + 1],
                    in1=o2[b // 2, h][:, t, b % 2, :],
                    op0=ALU.add,
                    op1=ALU.mult,
                )

        tr = {}

        def turn_out(b, h, i):
            if True:
                bank = psum.tile([P, 4, P], F32, name="t_bank", bufs=3)
                for t in range(4):
                    nc.tensor.matmul(
                        bank[:, t, :], lhsT=o1a[b][:, h, i, t, :], rhs=ident[:], start=True, stop=False, is_transpose=True
                    )
                    nc.tensor.matmul(
                        bank[:, t, :],
                        lhsT=fused[b][:, h, t, i * P : (i + 1) * P],
                        rhs=ident[:],
                        start=False,
                        stop=True,
                        is_transpose=True,
                    )
                tr[b, h, i] = bank

        def store(b, h, i):
            if True:
                rows = work.tile([P, W], F32, name="rows", bufs=6)
                dst = rows[:].rearrange("n (m t) -> n m t", t=4)
                src = tr[b, h, i][:].rearrange("n t m -> n m t")
                if (b, h, i) in EVAC_V:
                    nc.vector.tensor_copy(out=dst, in_=src)
                else:
                    nc.scalar.copy(out=dst, in_=src)
                n0 = b * TB + i * P
                nc.sync.dma_start(out=out[n0 : n0 + P, h * W : (h + 1) * W], in_=rows[:])

        turn_x(0, 0)
        widen_vectors()
        turn_x(0, 1)
        turn_x(1, 1)
        gate_x(0, 0)
        group_w1(1, 0)
        turn_x(1, 0)
        gate_x(0, 1)
        quant_x(0, 0)
        quant_w1(1, 0)
        group_w1(0, 0)
        gate_x(1, 1)
        quant_x(0, 1)
        group_w1(1, 1)
        turn_x(2, 0)
        gate_x(1, 0)
        turn_x(3, 1)
        group_w1(0, 1)
        quant_w1(1, 1)
        turn_x(2, 1)
        quant_x(1, 0)
        mul_z1(1, 1)
        gate_x(3, 1)
        turn_x(3, 0)
        widen_w2(1, 0)
        gain_z1(1, 1)
        quant_w1(0, 0)
        widen_w2(0, 1)
        widen_w2(1, 1)
        mul_z1(0, 1)
        gate_x(3, 0)
        quant_x(3, 0)
        gate_x(2, 0)
        widen_w2(0, 0)
        gain_z1(0, 1)
        mul_z1(3, 1)
        gain_z1(3, 1)
        linear_z1(1, 1)
        gate_x(2, 1)
        linear_z1(3, 1)
        group_w2(1, 1)
        group_w2(1, 0)
        linear_z1(0, 1)
        quant_x(2, 0)
        quant_w2(1, 1)
        quant_w2(1, 0)
        quant_x(1, 1)
        mul_z1(2, 1)
        weigh_z1(3, 1)
        weigh_z1(1, 1)
        mul_z2(0, 1, 0)
        quant_u(3, 1)
        quant_u(1, 1)
        mul_z2(0, 1, 1)
        quant_x(2, 1)
        quant_x(3, 1)
        gain_z1(2, 1)
        group_wf(1)
        mul_z2(1, 1, 1)
        mul_z2(1, 1, 0)
        quant_wf(1)
        mul_f(1, 1)
        use_z2(0, 1, 0)
        use_z2(0, 1, 1)
        use_z2(1, 1, 1)
        quant_w1(0, 1)
        use_z2(1, 1, 0)
        mul_z1(3, 0)
        mul_f(3, 1)
        linear_z1(2, 1)
        fuse(1, 1)
        turn_out(1, 1, 0)
        mul_z1(2, 0)
        turn_out(1, 1, 1)
        quant_u(0, 1)
        gain_z1(3, 0)
        group_w2(0, 0)
        mul_z1(0, 0)
        fuse(3, 1)
        gain_z1(2, 0)
        quant_w2(0, 0)
        group_w2(0, 1)
        linear_z1(2, 0)
        linear_z1(3, 0)
        quant_w2(0, 1)
        mul_z2(1, 0, 0)
        quant_u(2, 1)
        weigh_z1(0, 1)
        mul_f(0, 1)
        mul_z1(1, 0)
        gain_z1(0, 0)
        weigh_z1(2, 1)
        mul_f(2, 1)
        fuse(0, 1)
        use_z2(1, 0, 0)
        linear_z1(0, 0)
        fuse(2, 1)
        weigh_z1(3, 0)
        turn_out(0, 1, 1)
        store(1, 1, 0)
        quant_u(2, 0)
        turn_out(0, 1, 0)
        mul_z2(1, 0, 1)
        turn_out(2, 1, 1)
        store(1, 1, 1)
        group_wf(0)
        store(0, 1, 1)
        turn_out(2, 1, 0)
        quant_u(3, 0)
        quant_wf(0)
        store(0, 1, 0)
        use_z2(1, 0, 1)
        gain_z1(1, 0)
        mul_z2(0, 0, 1)
        linear_z1(1, 0)
        mul_f(2, 0)
        turn_out(3, 1, 1)
        weigh_z1(2, 0)
        turn_out(3, 1, 0)
        fuse(2, 0)
        store(2, 1, 0)
        mul_f(3, 0)
        store(2, 1, 1)
        quant_u(1, 0)
        store(3, 1, 1)
        fuse(3, 0)
        turn_out(2, 0, 1)
        turn_out(2, 0, 0)
        use_z2(0, 0, 1)
        store(3, 1, 0)
        weigh_z1(1, 0)
        store(2, 0, 1)
        mul_z2(0, 0, 0)
        use_z2(0, 0, 0)
        mul_f(1, 0)
        turn_out(3, 0, 1)
        store(3, 0, 1)
        weigh_z1(0, 0)
        turn_out(3, 0, 0)
        store(3, 0, 0)
        quant_u(0, 0)
        mul_f(0, 0)
        fuse(1, 0)
        store(2, 0, 0)
        turn_out(1, 0, 1)
        store(1, 0, 1)
        turn_out(1, 0, 0)
        store(1, 0, 0)
        fuse(0, 0)
        turn_out(0, 0, 1)
        store(0, 0, 1)
        turn_out(0, 0, 0)
        store(0, 0, 0)
